import numpy as np
import ml_dtypes


def mxq(x, axis, fmt="e4m3"):
    dtype, down = {"e4m3": (ml_dtypes.float8_e4m3fn, 7), "e5m2": (ml_dtypes.float8_e5m2, 14)}[fmt]
    v = np.moveaxis(np.asarray(x, np.float32).astype(ml_dtypes.bfloat16).astype(np.float64), axis, -1)
    blocks = v.reshape(v.shape[:-1] + (-1, 32))
    amax = np.abs(blocks).max(-1, keepdims=True)
    byte = np.maximum(np.where(amax > 0, np.frexp(amax)[1] - 1 + 127, 0) - down, 1)
    scale = np.exp2(byte - 127.0)
    codes = (blocks / scale).astype(np.float32).astype(dtype).astype(np.float64)
    return np.moveaxis((codes * scale).reshape(v.shape), -1, axis)


WIDE = False


def mx_kscale(k):
    if not WIDE:
        return np.ones(k)
    levels = np.array([30, -30])
    if k % 512:
        return np.exp2(np.random.permutation(np.resize(levels, k // 32))).repeat(32)
    a = np.empty((k // 512, 16))
    for p in range(k // 512):
        a[p, :8] = np.random.permutation(np.resize(levels, 8))
        for g in range(8):
            far = levels[np.abs(levels - a[p, g]) >= 10]
            a[p, g + 8] = far[np.random.randint(len(far))]
    return np.exp2(a.ravel()).repeat(32)


BF16 = ml_dtypes.bfloat16


def bf(x):
    return np.asarray(x, np.float32).astype(BF16)


def f64(x):
    return np.asarray(x).astype(np.float64)


E2M1 = np.array([0.0, 0.5, 1.0, 1.5, 2.0, 3.0, 4.0, 6.0, -0.0, -0.5, -1.0, -1.5, -2.0, -3.0, -4.0, -6.0])


def pack_weight(w, fmt):
    k, n = w.shape
    w = f64(bf(w)).reshape(k // 32, 32, n)
    amax = np.abs(w).max(1)
    if fmt in ("e4m3", "e5m2"):
        byte = np.frexp(amax)[1] - 1 + 127 - (7 if fmt == "e4m3" else 14)
    else:
        mant, ex = np.frexp(amax / 6.0)
        byte = np.where(mant > 0.5, ex, ex - 1) + 127
    byte = np.clip(np.where(amax > 0, byte, 1), 1, 254)
    scaled = (w * np.exp2(127.0 - byte)[:, None, :]).reshape(k, n).astype(np.float32)
    by_word = np.ascontiguousarray(scaled.reshape(k // 512, 128, 4, n).transpose(0, 1, 3, 2))
    if fmt in ("e4m3", "e5m2"):
        words = by_word.astype(ml_dtypes.float8_e4m3fn if fmt == "e4m3" else ml_dtypes.float8_e5m2).view(np.uint8)
    else:
        c = by_word.astype(ml_dtypes.float4_e2m1fn).view(np.uint8) & 0xF
        words = c[..., 0::2] | (c[..., 1::2] << 4)
    return np.ascontiguousarray(words), np.ascontiguousarray(byte.astype(np.uint8).reshape(k // 512, 16, n))


def unpack_weight(words, scales, fmt):
    g, p, n, _ = words.shape
    if fmt in ("e4m3", "e5m2"):
        vals = np.ascontiguousarray(words).view(ml_dtypes.float8_e4m3fn if fmt == "e4m3" else ml_dtypes.float8_e5m2).astype(np.float64)
    else:
        nib = np.empty((g, p, n, 4), np.uint8)
        nib[..., 0::2] = words & 0xF
        nib[..., 1::2] = words >> 4
        vals = E2M1[nib]
    vals = vals * np.repeat(np.exp2(scales.astype(np.float64) - 127.0), 8, axis=1)[..., None]
    return vals.transpose(0, 1, 3, 2).reshape(g * 512, n)


B, N1, N2, D = 1024, 2048, 1024, 1536


def setup_inputs():
    s, u = mx_kscale(N1), mx_kscale(N2)
    spread = np.exp(0.3 * np.random.standard_normal(D))
    G = np.random.standard_t(5, (N1, D)) * spread
    phi = 0.8 * np.random.standard_normal((N2, D)) * spread
    var = np.mean(G ** 2, axis=0) + np.mean(phi ** 2, axis=0) * N1 / N2
    xi = np.random.standard_normal((B, N1)) / np.sqrt(N1)
    zeta = np.random.standard_normal((B, N2)) * np.sqrt(N1) / N2
    G_words, G_scales = pack_weight(G * s[:, None], "e5m2")
    return {"xi": bf(xi / s),
            "g_words": G_words,
            "g_scales": G_scales,
            "zeta": bf(zeta / u),
            "phi": bf(phi * u[:, None]),
            "inv_sd": bf(1.0 / np.sqrt(var))}


def reference(xi, g_words, g_scales, zeta, phi, inv_sd):
    G = unpack_weight(g_words, g_scales, "e5m2")
    main = mxq(f64(xi), 1, "e4m3") @ G
    aux = mxq(f64(zeta), 1, "e4m3") @ mxq(f64(phi), 0, "e4m3")
    T = (main + aux) * f64(inv_sd)
    sup_t = np.max(np.abs(T), axis=1)
    return T, sup_t

from contextlib import ExitStack

import concourse.mybir as mybir
from concourse.masks import make_identity

B, N1, N2, D = 1024, 2048, 1024, 1536
FLOPS = 2 * B * (N1 + N2) * D

F32 = mybir.dt.float32
BF16 = mybir.dt.bfloat16
I32 = mybir.dt.int32
U32 = mybir.dt.uint32
U8 = mybir.dt.uint8
E4M3X4 = mybir.dt.float8_e4m3fn_x4
E5M2X4 = mybir.dt.float8_e5m2_x4
ALU = mybir.AluOpType

P = 128
PACK = 4
K_PASS = P * PACK
COLS = 512
TILES = B // P
CHUNKS = D // COLS
MAIN = N1 // K_PASS
AUX = N2 // K_PASS
PAIRS = (MAIN + AUX) // 2
ACC_BANKS = 5
TR_BANKS = 3


def tile_multiplier_bootstrap_supt_e4_kernel(tc, xi, g_words, g_scales, zeta, phi, inv_sd, out_0, out_1):
    nc = tc.nc
    with ExitStack() as ctx:
        keep = ctx.enter_context(tc.tile_pool(name="keep", bufs=1))
        psum = ctx.enter_context(tc.psum_pool(name="psum", bufs=1))
        ctx.enter_context(tc.manual_schedule())

        def sb(name, shape, dtype):
            return keep.tile(shape, dtype, name=name, align_bytes=64)

        xi_rows = xi.rearrange("(p i) k -> i p k", i=TILES)
        zeta_rows = zeta.rearrange("(p i) k -> i p k", i=TILES)
        t_rows = out_0.rearrange("(p i) j -> i p j", i=TILES)

        ident = sb("ident", [P, P], F32)
        ones = sb("ones", [P, P], BF16)
        inv_row = sb("inv_row", [P, D], BF16)
        inv = [sb("inv%d" % n, [P, COLS], F32) for n in range(CHUNKS)]
        x_raw = [sb("x_raw%d" % i, [P, N1], BF16) for i in range(TILES)]
        z_raw = [sb("z_raw%d" % i, [P, N2], BF16) for i in range(TILES)]
        m_codes = [[sb("m_codes%d_%d" % (i, h), [P, 2 * P], U32) for h in range(PAIRS)] for i in range(TILES)]
        m_scales = [[sb("m_scales%d_%d" % (i, h), [P, 2 * P], U8) for h in range(PAIRS)] for i in range(TILES)]
        g_codes = [[sb("g_codes%d_%d" % (g, n), [P, COLS], U32) for n in range(CHUNKS)] for g in range(MAIN)]
        g_plane_first = sb("g_plane_first", [P, MAIN, COLS], U8)
        g_plane_rest = sb("g_plane_rest", [P, MAIN, D - COLS], U8)
        p_raw = [[sb("p_raw%d_%d" % (g, n), [P, PACK, COLS], BF16) for n in range(CHUNKS)] for g in range(AUX)]
        p_codes = [[sb("p_codes%d_%d" % (g, n), [P, COLS], U32) for n in range(CHUNKS)] for g in range(AUX)]
        p_scales = [[sb("p_scales%d_%d" % (g, n), [P, COLS], U8) for n in range(CHUNKS)] for g in range(AUX)]
        p_grouped = [sb("p_grouped%d" % s, [P, COLS, PACK], BF16) for s in range(2)]
        m_grouped = [sb("m_grouped%d" % s, [P, 2, P, PACK], BF16) for s in range(4)]
        t_out = [[sb("t_out%d_%d" % (i, n), [P, COLS + 8], F32) for n in range(CHUNKS)] for i in range(TILES)]
        sup = sb("sup", [P, TILES], F32)
        acc_banks = [psum.tile([P, COLS], F32, name="acc%d" % s) for s in range(ACC_BANKS)]
        tr_banks = [psum.tile([P, 2, 2, P], F32, name="tr%d" % s) for s in range(TR_BANKS)]

        def cols(n):
            return slice(n * COLS, (n + 1) * COLS)

        def load_x(i, h):
            ks = slice(2 * K_PASS * h, 2 * K_PASS * (h + 1))
            nc.sync.dma_start(out=x_raw[i][:, ks], in_=xi_rows[i][:, ks])

        def load_x_all(i):
            nc.sync.dma_start(out=x_raw[i][:], in_=xi_rows[i])

        def load_z(i):
            nc.sync.dma_start(out=z_raw[i][:], in_=zeta_rows[i])

        def load_g(g, n):
            src = g_words[g].rearrange("p n t -> p (n t)")[:, PACK * COLS * n:PACK * COLS * (n + 1)]
            nc.sync.dma_start(out=g_codes[g][n][:].bitcast(I32), in_=src.bitcast(I32))

        def load_p(g, n):
            src = phi[g * K_PASS:(g + 1) * K_PASS, cols(n)].rearrange("(p t) n -> p t n", t=PACK)
            nc.sync.dma_start(out=p_raw[g][n][:], in_=src)

        def load_plane(queue, plane, c0, c1):
            for q in range(4):
                src = g_scales[:, 4 * q:4 * q + 4, c0:c1].rearrange("g r n -> r g n")
                queue.dma_start(out=plane[32 * q:32 * q + 4].bitcast(I32), in_=src.bitcast(I32))

        def g_scale(g, n):
            if n == 0:
                return g_plane_first[:, g, :]
            return g_plane_rest[:, g, (n - 1) * COLS:n * COLS]

        turns = []
        units = []
        pending = []

        def turn(i, h):
            s = len(turns)
            turns.append((i, h))
            bank = tr_banks[s % TR_BANKS]
            grouped = m_grouped[s % len(m_grouped)]
            if h < MAIN // 2:
                words = x_raw[i][:].bitcast(F32)[:, K_PASS * h:K_PASS * (h + 1)]
            else:
                words = z_raw[i][:].bitcast(F32)
            for g in range(2):
                for u in range(2):
                    nc.tensor.transpose(bank[:, g, u, :], words[:, 2 * P * g + u:2 * P * (g + 1):2], ident[:])
            nc.scalar.copy(out=grouped[:].bitcast(F32), in_=bank[:].rearrange("p g u r -> p g r u"))

        def quant(i, h):
            grouped = m_grouped[turns.index((i, h)) % len(m_grouped)]
            nc.vector.quantize_mx(
                out=m_codes[i][h][:].bitcast(E4M3X4),
                scales=m_scales[i][h][:],
                in_=grouped[:].rearrange("p g r t -> p (g r t)"),
            )

        def weave_p(copy, g, n, part, parts):
            w = COLS // parts
            cs = slice(part * w, (part + 1) * w)
            copy(out=p_grouped[g][:, cs, :], in_=p_raw[g][n][:, :, cs].rearrange("p t n -> p n t"))

        def quant_p(g, n):
            nc.vector.quantize_mx(
                out=p_codes[g][n][:].bitcast(E4M3X4),
                scales=p_scales[g][n][:],
                in_=p_grouped[g][:].rearrange("p n t -> p (n t)"),
            )

        def passes(i, n, first, last):
            if first == 0:
                units.append((i, n))
            acc = acc_banks[units.index((i, n)) % ACC_BANKS]
            for c in range(first, last):
                rows = slice((c % 2) * P, (c % 2 + 1) * P)
                if c < MAIN:
                    rhs, rhs_scale = g_codes[c][n][:].bitcast(E5M2X4), g_scale(c, n)
                else:
                    rhs, rhs_scale = p_codes[c - MAIN][n][:].bitcast(E4M3X4), p_scales[c - MAIN][n][:]
                nc.tensor.matmul_mx(
                    out=acc[:],
                    lhsT=m_codes[i][c // 2][:, rows].bitcast(E4M3X4),
                    lhsT_scale=m_scales[i][c // 2][:, rows],
                    rhs=rhs,
                    rhs_scale=rhs_scale,
                    start=(c == 0),
                    stop=(c == MAIN + AUX - 1),
                )

        def reduce_pending():
            for i, n in pending:
                width = COLS if n == 0 else COLS + 1
                dst = t_out[i][n + 1][:, COLS:COLS + 1] if n + 1 < CHUNKS else sup[:, i:i + 1]
                nc.vector.tensor_reduce(out=dst, in_=t_out[i][n][:, :width], axis=mybir.AxisListType.X,
                                        op=ALU.max, apply_absolute_value=True)
            pending.clear()

        def scale_out(i, n):
            acc = acc_banks[units.index((i, n)) % ACC_BANKS]
            nc.vector.tensor_tensor(out=t_out[i][n][:, :COLS], in0=acc[:], in1=inv[n][:], op=ALU.mult)
            reduce_pending()
            pending.append((i, n))

        def store(i, n):
            nc.sync.dma_start(out=t_rows[i][:, cols(n)], in_=t_out[i][n][:, :COLS])

        def spread_inv(n):
            acc = acc_banks[ACC_BANKS - 1 - n]
            nc.tensor.matmul(acc[:], ones[:], inv_row[:, cols(n)], start=True, stop=True)
            nc.scalar.copy(out=inv[n][:], in_=acc[:])

        nc.vector.memset(g_plane_first[:].rearrange("p g n -> p (g n)").bitcast(I32), 0)
        nc.vector.memset(inv_row[:].bitcast(I32), 0)
        nc.vector.memset(g_plane_rest[:].rearrange("p g n -> p (g n)").bitcast(I32), 0)
        make_identity(nc, ident[:])
        nc.gpsimd.memset(ones[:], 1.0)
        nc.gpsimd.dma_start(out=inv_row[0:1, :], in_=inv_sd.unsqueeze(0))

        load_x(0, 0)
        load_x(0, 1)
        load_x_all(1)
        load_plane(nc.sync, g_plane_first, 0, COLS)
        load_g(0, 0)
        load_x_all(2)
        load_g(1, 0)
        load_g(2, 0)
        load_x_all(3)
        load_g(3, 0)
        load_x_all(4)
        load_p(0, 0)
        load_z(0)
        load_z(1)
        load_p(1, 0)
        for i in range(2, 5):
            load_z(i)
        load_x_all(5)
        load_z(5)
        load_plane(nc.sync, g_plane_rest, COLS, D)
        for g in range(MAIN):
            load_g(g, 1)
        load_p(0, 1)
        load_p(1, 1)
        load_x_all(6)
        load_z(6)
        load_x_all(7)
        load_z(7)
        for g in range(MAIN):
            load_g(g, 2)
        load_p(0, 2)
        load_p(1, 2)

        def tq(*pieces):
            for i, h in pieces:
                turn(i, h)
            for i, h in pieces:
                quant(i, h)

        def whole(i, n):
            passes(i, n, 0, ALL)
            scale_out(i, n)

        def finish(i, n):
            passes(i, n, MAIN, ALL)
            scale_out(i, n)

        def weave_s(g, n):
            for part in range(2):
                weave_p(nc.scalar.copy, g, n, part, 2)

        ALL = MAIN + AUX
        tq((0, 0), (0, 1))
        tq((1, 0), (1, 1))
        for n in range(CHUNKS):
            spread_inv(n)
        passes(0, 0, 0, 1)
        passes(1, 0, 0, 1)
        tq((2, 0), (2, 1))
        passes(0, 0, 1, 3)
        passes(1, 0, 1, 3)
        passes(2, 0, 0, 1)
        tq((3, 0), (3, 1))
        passes(0, 0, 3, 4)
        passes(1, 0, 3, 4)
        passes(2, 0, 1, 4)
        weave_p(nc.vector.tensor_copy, 0, 0, 0, 1)
        tq((4, 0), (4, 1))
        quant_p(0, 0)
        weave_p(nc.vector.tensor_copy, 1, 0, 0, 1)
        passes(3, 0, 0, MAIN)
        tq((0, 2), (1, 2))
        quant_p(1, 0)
        passes(4, 0, 0, MAIN)
        tq((2, 2), (3, 2), (4, 2))
        finish(0, 0)
        finish(1, 0)
        tq((5, 0), (5, 1), (5, 2))
        finish(2, 0)
        finish(3, 0)
        finish(4, 0)
        whole(5, 0)
        weave_s(0, 1)
        passes(0, 1, 0, MAIN)
        passes(1, 1, 0, MAIN)
        quant_p(0, 1)
        weave_s(1, 1)
        passes(2, 1, 0, MAIN)
        passes(3, 1, 0, MAIN)
        quant_p(1, 1)
        tq((6, 0), (6, 1), (6, 2))
        finish(0, 1)
        finish(1, 1)
        finish(2, 1)
        finish(3, 1)
        tq((7, 0), (7, 1), (7, 2))
        whole(6, 0)
        weave_s(0, 2)
        whole(4, 1)
        whole(7, 0)
        quant_p(0, 2)
        weave_s(1, 2)
        whole(5, 1)
        whole(6, 1)
        quant_p(1, 2)
        whole(7, 1)
        for i in range(TILES):
            whole(i, 2)
            reduce_pending()

        for i, n in units:
            store(i, n)
        nc.sync.dma_start(out=out_1.rearrange("(p i) -> p i", i=TILES), in_=sup[:])
